import numpy as np
import ml_dtypes


def mxq(x, axis, fmt="e4m3"):
    dtype, down = {"e4m3": (ml_dtypes.float8_e4m3fn, 7), "e5m2": (ml_dtypes.float8_e5m2, 14)}[fmt]
    v = np.moveaxis(np.asarray(x, np.float32).astype(ml_dtypes.bfloat16).astype(np.float64), axis, -1)
    blocks = v.reshape(v.shape[:-1] + (-1, 32))
    amax = np.abs(blocks).max(-1, keepdims=True)
    byte = np.maximum(np.where(amax > 0, np.frexp(amax)[1] - 1 + 127, 0) - down, 1)
    scale = np.exp2(byte - 127.0)
    codes = (blocks / scale).astype(np.float32).astype(dtype).astype(np.float64)
    return np.moveaxis((codes * scale).reshape(v.shape), -1, axis)


WIDE = False


def mx_kscale(k, group=512):
    if not WIDE:
        return np.ones(k)
    levels = np.array([10, -10, 5, -5, 0])
    if group != 512:
        return np.exp2(np.random.permutation(np.resize(levels, k // group))).repeat(group)
    if k % 512:
        return np.exp2(np.random.permutation(np.resize(levels, k // 32))).repeat(32)
    a = np.empty((k // 512, 16))
    for p in range(k // 512):
        a[p, :8] = np.random.permutation(np.resize(levels, 8))
        for g in range(8):
            far = levels[np.abs(levels - a[p, g]) >= 10]
            a[p, g + 8] = far[np.random.randint(len(far))]
    return np.exp2(a.ravel()).repeat(32)


def f64(x):
    return np.asarray(x).astype(np.float64)


H, D, N = 4, 256, 512


def setup_inputs():
    n = np.random.standard_normal
    s = mx_kscale(D, 0)[:, None]
    S = n((H, D, 128))
    S[:, :, 127] = np.random.uniform(0.5, 1.5, (H, D))
    return {
        "q": n((H, D, N)).astype(np.float32),
        "qa": (np.random.uniform(0.5, 2.0, (D, 1)) * s).astype(np.float32),
        "S": (S / s).astype(np.float32),
        "og": n((H, N, 128)).astype(np.float32),
    }


def reference(q, qa, S, og):
    fq = (np.maximum(f64(q), 0.0) + 0.125) * f64(qa)
    y = mxq(fq, 1, "e4m3").transpose(0, 2, 1) @ mxq(f64(S), 1, "e4m3")
    y = y / y[:, :, 127:128]
    y = y / (1.0 + np.exp(-f64(og)))
    return y

@@ -1,0 +1,185 @@
+from contextlib import ExitStack
+
+import concourse.mybir as mybir
+
+H, D, N, E = 4, 256, 512, 128
+FLOPS = 2 * H * D * N * E
+
+F32 = mybir.dt.float32
+BF16 = mybir.dt.bfloat16
+U32 = mybir.dt.uint32
+U8 = mybir.dt.uint8
+FP8X4 = mybir.dt.float8_e4m3fn_x4
+ALU = mybir.AluOpType
+ACT = mybir.ActivationFunctionType
+
+P = 128
+PACK = 4
+ROWS = D // PACK
+DEAL = N // P
+EARLY = 8
+SHIFT = 0.125
+FAR = 2.0 ** 127
+
+
+def tile_rows_read_relu1_norm_gate_kernel(tc, q, qa, S, og, out):
+    nc = tc.nc
+    q_rows = q.rearrange("h d n -> (h d) n")
+    s_rows = S.rearrange("h d e -> (h d) e")
+    qa_rows = qa.rearrange("(p j) o -> p (j o)", j=PACK)
+
+    with ExitStack() as ctx:
+        sb = ctx.enter_context(tc.tile_pool(name="sb", bufs=1))
+        ps = ctx.enter_context(tc.psum_pool(name="ps", bufs=1))
+        ctx.enter_context(tc.manual_schedule())
+
+        weight = sb.tile([P, PACK], F32, name="weight")
+        floor = sb.tile([P, PACK], F32, name="floor")
+        side = sb.tile([P, PACK], F32, name="side")
+        low = sb.tile([P, PACK], F32, name="low")
+        high = sb.tile([P, PACK], F32, name="high")
+        q_raw = [[sb.tile([P, N], F32, name=f"q_raw{g}{j}") for j in range(PACK)] for g in range(2)]
+        s_raw = [sb.tile([P, PACK, E], F32, name=f"s_raw{g}") for g in range(2)]
+        og_raw = [sb.tile([P, N], F32, name=f"og_raw{h}") for h in range(H)]
+        gate = [sb.tile([P, N], F32, name=f"gate{h}") for h in range(H)]
+        mapped = [sb.tile([P, PACK, N], BF16, name=f"mapped{g}", align_bytes=64) for g in range(2)]
+        q_packed = [sb.tile([P, DEAL * P * PACK], BF16, name=f"q_packed{g}", align_bytes=64) for g in range(2)]
+        s_packed = [sb.tile([P, E * PACK], BF16, name=f"s_packed{g}", align_bytes=64) for g in range(2)]
+        q_codes = [sb.tile([P, N], U32, name=f"q_codes{g}", align_bytes=64) for g in range(2)]
+        q_scales = [sb.tile([P, N], U8, name=f"q_scales{g}", align_bytes=64) for g in range(2)]
+        s_codes = [sb.tile([P, E], U32, name=f"s_codes{g}", align_bytes=64) for g in range(2)]
+        s_scales = [sb.tile([P, E], U8, name=f"s_scales{g}", align_bytes=64) for g in range(2)]
+        inverse = [sb.tile([P, DEAL], F32, name=f"inverse{h}") for h in range(H)]
+        result = [sb.tile([P, N], F32, name=f"result{h}") for h in range(H)]
+        sums = [ps.tile([P, DEAL, E], F32, name=f"sums{h}") for h in range(H)]
+
+        def dealt(x, h):
+            return x[h].rearrange("(s r) e -> s (r e)", r=DEAL)
+
+        def load_q(g, j):
+            src = q_rows[2 * D * g : 2 * D * (g + 1), :].rearrange("(p j) n -> p j n", j=PACK)
+            nc.sync.dma_start(out=q_raw[g][j][:], in_=src[:, j, :])
+
+        def load_s(g):
+            src = s_rows[2 * D * g : 2 * D * (g + 1), :].rearrange("(p j) e -> p j e", j=PACK)
+            nc.sync.dma_start(out=s_raw[g][:], in_=src)
+
+        def load_og(h, first=0):
+            nc.sync.dma_start(out=og_raw[h][:, first:], in_=dealt(og, h)[:, first:])
+
+        def sigmoid(h, first=0, last=N):
+            nc.scalar.activation(out=gate[h][:, first:last], in_=og_raw[h][:, first:last], func=ACT.Sigmoid)
+
+        def affine_scalar(g, j):
+            nc.scalar.activation(out=mapped[g][:, j, :], in_=q_raw[g][j][:], func=ACT.Identity,
+                                 scale=weight[:, j : j + 1], bias=floor[:, j : j + 1])
+
+        def affine_vector(g, j):
+            nc.vector.tensor_scalar(out=mapped[g][:, j, :], in0=q_raw[g][j][:], scalar1=SHIFT,
+                                    scalar2=weight[:, j : j + 1], op0=ALU.add, op1=ALU.mult)
+
+        def clamp(g, j):
+            nc.vector.tensor_scalar(out=mapped[g][:, j, :], in0=mapped[g][:, j, :], scalar1=low[:, j : j + 1],
+                                    scalar2=high[:, j : j + 1], op0=ALU.max, op1=ALU.min)
+
+        def pack_q(g):
+            nc.vector.tensor_copy(
+                out=q_packed[g][:].rearrange("p (r a b j) -> p a j b r", r=DEAL, b=2, j=PACK),
+                in_=mapped[g][:].rearrange("p j (a b r) -> p a j b r", b=2, r=DEAL))
+
+        def pack_s(g):
+            nc.scalar.copy(
+                out=s_packed[g][:].rearrange("p (c i j) -> p c j i", i=4, j=PACK),
+                in_=s_raw[g][:].rearrange("p j (c i) -> p c j i", i=4))
+
+        def quantize_q(g, half):
+            w = N // 2
+            nc.vector.quantize_mx(out=q_codes[g][:, half * w : (half + 1) * w].bitcast(FP8X4),
+                                  scales=q_scales[g][:, half * w : (half + 1) * w],
+                                  in_=q_packed[g][:, half * w * PACK : (half + 1) * w * PACK])
+
+        def quantize_s(g):
+            nc.vector.quantize_mx(out=s_codes[g][:].bitcast(FP8X4), scales=s_scales[g][:], in_=s_packed[g][:])
+
+        def products(g):
+            for r in range(DEAL):
+                cols = slice(r * P, (r + 1) * P)
+                for c in range(2):
+                    rows = slice(c * ROWS, (c + 1) * ROWS)
+                    nc.tensor.matmul_mx(out=sums[2 * g + c][:, r, :],
+                                        lhsT=q_codes[g][rows, cols].bitcast(FP8X4), lhsT_scale=q_scales[g][rows, cols],
+                                        rhs=s_codes[g][rows, :].bitcast(FP8X4), rhs_scale=s_scales[g][rows, :],
+                                        start=True, stop=True)
+
+        def invert(h):
+            nc.vector.reciprocal(out=inverse[h][:], in_=sums[h][:, :, E - 1])
+
+        def finish(h, r):
+            cols = slice(r * E, (r + 1) * E)
+            nc.vector.scalar_tensor_tensor(out=result[h][:, cols], in0=sums[h][:, r, :], scalar=inverse[h][:, r : r + 1],
+                                           in1=gate[h][:, cols], op0=ALU.mult, op1=ALU.mult)
+
+        def store(h):
+            nc.sync.dma_start(out=dealt(out, h), in_=result[h][:])
+
+        for c in range(2):
+            nc.scalar.dma_start(out=weight[c * ROWS : (c + 1) * ROWS, :], in_=qa_rows)
+        nc.scalar.dma_start(out=og_raw[0][:, :EARLY], in_=dealt(og, 0)[:, :EARLY])
+        for j in range(PACK):
+            load_q(0, j)
+        load_s(0)
+        for j in range(PACK - 1):
+            load_q(1, j)
+        load_og(0, EARLY)
+        load_q(1, PACK - 1)
+        load_s(1)
+        for h in range(1, H):
+            load_og(h)
+
+        sigmoid(0, 0, EARLY)
+        nc.vector.tensor_scalar(out=floor[:], in0=weight[:], scalar1=SHIFT, scalar2=None, op0=ALU.mult)
+        nc.vector.tensor_scalar(out=side[:], in0=weight[:], scalar1=0.0, scalar2=0.5, op0=ALU.is_ge, op1=ALU.subtract)
+        nc.vector.scalar_tensor_tensor(out=low[:], in0=side[:], scalar=FAR, in1=floor[:], op0=ALU.mult, op1=ALU.min)
+        nc.vector.scalar_tensor_tensor(out=high[:], in0=side[:], scalar=FAR, in1=floor[:], op0=ALU.mult, op1=ALU.max)
+
+        for j in range(PACK - 1):
+            affine_scalar(0, j)
+            clamp(0, j)
+        affine_vector(0, PACK - 1)
+        clamp(0, PACK - 1)
+        pack_q(0)
+        pack_s(0)
+        quantize_s(0)
+        quantize_q(0, 0)
+        quantize_q(0, 1)
+        products(0)
+        for j in range(PACK - 1):
+            affine_scalar(1, j)
+            clamp(1, j)
+        invert(0)
+        invert(1)
+        sigmoid(0, EARLY)
+        affine_scalar(1, PACK - 1)
+        for r in range(DEAL - 1):
+            finish(0, r)
+        clamp(1, PACK - 1)
+        finish(0, DEAL - 1)
+        store(0)
+        pack_q(1)
+        pack_s(1)
+        for h in range(1, H):
+            sigmoid(h)
+        quantize_s(1)
+        finish(1, 0)
+        quantize_q(1, 0)
+        quantize_q(1, 1)
+        products(1)
+        for r in range(1, DEAL):
+            finish(1, r)
+        store(1)
+        invert(2)
+        invert(3)
+        for h in range(2, H):
+            for r in range(DEAL):
+                finish(h, r)
+            store(h)

@@ -17,6 +17,7 @@ P = 128
 PACK = 4
 ROWS = D // PACK
 DEAL = N // P
+HALF = N // 2
 EARLY = 8
 SHIFT = 0.125
 FAR = 2.0 ** 127
@@ -38,7 +39,7 @@ def tile_rows_read_relu1_norm_gate_kernel(tc, q, qa, S, og, out):
         side = sb.tile([P, PACK], F32, name="side")
         low = sb.tile([P, PACK], F32, name="low")
         high = sb.tile([P, PACK], F32, name="high")
-        q_raw = [[sb.tile([P, N], F32, name=f"q_raw{g}{j}") for j in range(PACK)] for g in range(2)]
+        q_raw = [sb.tile([P, PACK, N], F32, name=f"q_raw{g}") for g in range(2)]
         s_raw = [sb.tile([P, PACK, E], F32, name=f"s_raw{g}") for g in range(2)]
         og_raw = [sb.tile([P, N], F32, name=f"og_raw{h}") for h in range(H)]
         gate = [sb.tile([P, N], F32, name=f"gate{h}") for h in range(H)]
@@ -56,9 +57,9 @@ def tile_rows_read_relu1_norm_gate_kernel(tc, q, qa, S, og, out):
         def dealt(x, h):
             return x[h].rearrange("(s r) e -> s (r e)", r=DEAL)
 
-        def load_q(g, j):
+        def load_q(g, places, first=0, last=N):
             src = q_rows[2 * D * g : 2 * D * (g + 1), :].rearrange("(p j) n -> p j n", j=PACK)
-            nc.sync.dma_start(out=q_raw[g][j][:], in_=src[:, j, :])
+            nc.sync.dma_start(out=q_raw[g][:, places, first:last], in_=src[:, places, first:last])
 
         def load_s(g):
             src = s_rows[2 * D * g : 2 * D * (g + 1), :].rearrange("(p j) e -> p j e", j=PACK)
@@ -70,41 +71,44 @@ def tile_rows_read_relu1_norm_gate_kernel(tc, q, qa, S, og, out):
         def sigmoid(h, first=0, last=N):
             nc.scalar.activation(out=gate[h][:, first:last], in_=og_raw[h][:, first:last], func=ACT.Sigmoid)
 
-        def affine_scalar(g, j):
-            nc.scalar.activation(out=mapped[g][:, j, :], in_=q_raw[g][j][:], func=ACT.Identity,
+        def affine_scalar(g, j, first=0):
+            nc.scalar.activation(out=mapped[g][:, j, first:], in_=q_raw[g][:, j, first:], func=ACT.Identity,
                                  scale=weight[:, j : j + 1], bias=floor[:, j : j + 1])
 
-        def affine_vector(g, j):
-            nc.vector.tensor_scalar(out=mapped[g][:, j, :], in0=q_raw[g][j][:], scalar1=SHIFT,
+        def affine_vector(g, j, last=N):
+            nc.vector.tensor_scalar(out=mapped[g][:, j, :last], in0=q_raw[g][:, j, :last], scalar1=SHIFT,
                                     scalar2=weight[:, j : j + 1], op0=ALU.add, op1=ALU.mult)
 
-        def clamp(g, j):
-            nc.vector.tensor_scalar(out=mapped[g][:, j, :], in0=mapped[g][:, j, :], scalar1=low[:, j : j + 1],
+        def clamp(g, j, first=0, last=N):
+            nc.vector.tensor_scalar(out=mapped[g][:, j, first:last], in0=mapped[g][:, j, first:last], scalar1=low[:, j : j + 1],
                                     scalar2=high[:, j : j + 1], op0=ALU.max, op1=ALU.min)
 
-        def pack_q(g):
+        def pack_q(g, tiles=DEAL, first=0, last=P // 2):
             nc.vector.tensor_copy(
-                out=q_packed[g][:].rearrange("p (r a b j) -> p a j b r", r=DEAL, b=2, j=PACK),
-                in_=mapped[g][:].rearrange("p j (a b r) -> p a j b r", b=2, r=DEAL))
+                out=q_packed[g][:].rearrange("p (r a b j) -> p a j b r", r=DEAL, b=2, j=PACK)[:, first:last, :, :, :tiles],
+                in_=mapped[g][:].rearrange("p j (a b r) -> p a j b r", b=2, r=DEAL)[:, first:last, :, :, :tiles])
+
+        def pack_q_scalar(g, r):
+            nc.scalar.copy(
+                out=q_packed[g][:].rearrange("p (r a b j) -> p r a j b", r=DEAL, b=2, j=PACK)[:, r, :, :, :],
+                in_=mapped[g][:].rearrange("p j (a b r) -> p r a j b", b=2, r=DEAL)[:, r, :, :, :])
 
         def pack_s(g):
             nc.scalar.copy(
                 out=s_packed[g][:].rearrange("p (c i j) -> p c j i", i=4, j=PACK),
                 in_=s_raw[g][:].rearrange("p j (c i) -> p c j i", i=4))
 
-        def quantize_q(g, half):
-            w = N // 2
-            nc.vector.quantize_mx(out=q_codes[g][:, half * w : (half + 1) * w].bitcast(FP8X4),
-                                  scales=q_scales[g][:, half * w : (half + 1) * w],
-                                  in_=q_packed[g][:, half * w * PACK : (half + 1) * w * PACK])
+        def quantize_q(g, first=0, last=N):
+            nc.vector.quantize_mx(out=q_codes[g][:, first:last].bitcast(FP8X4), scales=q_scales[g][:, first:last],
+                                  in_=q_packed[g][:, first * PACK : last * PACK])
 
         def quantize_s(g):
             nc.vector.quantize_mx(out=s_codes[g][:].bitcast(FP8X4), scales=s_scales[g][:], in_=s_packed[g][:])
 
-        def products(g):
-            for r in range(DEAL):
-                cols = slice(r * P, (r + 1) * P)
-                for c in range(2):
+        def products(g, tiles):
+            for c in range(2):
+                for r in tiles:
+                    cols = slice(r * P, (r + 1) * P)
                     rows = slice(c * ROWS, (c + 1) * ROWS)
                     nc.tensor.matmul_mx(out=sums[2 * g + c][:, r, :],
                                         lhsT=q_codes[g][rows, cols].bitcast(FP8X4), lhsT_scale=q_scales[g][rows, cols],
@@ -119,67 +123,71 @@ def tile_rows_read_relu1_norm_gate_kernel(tc, q, qa, S, og, out):
             nc.vector.scalar_tensor_tensor(out=result[h][:, cols], in0=sums[h][:, r, :], scalar=inverse[h][:, r : r + 1],
                                            in1=gate[h][:, cols], op0=ALU.mult, op1=ALU.mult)
 
-        def store(h):
-            nc.sync.dma_start(out=dealt(out, h), in_=result[h][:])
+        def store(h, half, queue):
+            cols = slice(half * HALF, (half + 1) * HALF)
+            queue.dma_start(out=dealt(out, h)[:, cols], in_=result[h][:, cols])
 
-        for c in range(2):
-            nc.scalar.dma_start(out=weight[c * ROWS : (c + 1) * ROWS, :], in_=qa_rows)
         nc.scalar.dma_start(out=og_raw[0][:, :EARLY], in_=dealt(og, 0)[:, :EARLY])
-        for j in range(PACK):
-            load_q(0, j)
+        load_q(0, slice(0, 2))
+        for c in range(2):
+            nc.sync.dma_start(out=weight[c * ROWS : (c + 1) * ROWS, :], in_=qa_rows)
+        load_q(0, 2)
+        load_q(0, 3, 0, HALF)
+        load_q(0, 3, HALF)
         load_s(0)
-        for j in range(PACK - 1):
+        for j in range(PACK):
             load_q(1, j)
-        load_og(0, EARLY)
-        load_q(1, PACK - 1)
         load_s(1)
+        load_og(0, EARLY)
         for h in range(1, H):
             load_og(h)
 
         sigmoid(0, 0, EARLY)
         nc.vector.tensor_scalar(out=floor[:], in0=weight[:], scalar1=SHIFT, scalar2=None, op0=ALU.mult)
         nc.vector.tensor_scalar(out=side[:], in0=weight[:], scalar1=0.0, scalar2=0.5, op0=ALU.is_ge, op1=ALU.subtract)
+        affine_vector(0, 0)
         nc.vector.scalar_tensor_tensor(out=low[:], in0=side[:], scalar=FAR, in1=floor[:], op0=ALU.mult, op1=ALU.min)
         nc.vector.scalar_tensor_tensor(out=high[:], in0=side[:], scalar=FAR, in1=floor[:], op0=ALU.mult, op1=ALU.max)
-
-        for j in range(PACK - 1):
-            affine_scalar(0, j)
-            clamp(0, j)
-        affine_vector(0, PACK - 1)
-        clamp(0, PACK - 1)
-        pack_q(0)
+        affine_scalar(0, 1)
+        affine_vector(0, 2)
+        affine_vector(0, 3, HALF)
+        affine_scalar(0, 3, HALF)
+        clamp(0, 0)
+        clamp(0, 1)
+        clamp(0, 2)
+        clamp(0, 3, 0, HALF)
+        clamp(0, 3, HALF)
+        pack_q(0, DEAL, 0, P // 4)
+        pack_q(0, DEAL, P // 4)
         pack_s(0)
-        quantize_s(0)
-        quantize_q(0, 0)
-        quantize_q(0, 1)
-        products(0)
         for j in range(PACK - 1):
             affine_scalar(1, j)
-            clamp(1, j)
-        invert(0)
-        invert(1)
-        sigmoid(0, EARLY)
-        affine_scalar(1, PACK - 1)
-        for r in range(DEAL - 1):
-            finish(0, r)
-        clamp(1, PACK - 1)
-        finish(0, DEAL - 1)
-        store(0)
-        pack_q(1)
+        affine_scalar(1, 3, HALF)
+        quantize_s(0)
+        quantize_q(0)
+        products(0, range(DEAL))
+        clamp(1, 0)
+        clamp(1, 1)
+        affine_vector(1, 3, HALF)
+        clamp(1, 2)
+        clamp(1, 3)
         pack_s(1)
+        pack_q(1, DEAL - 1)
+        pack_q_scalar(1, DEAL - 1)
+        sigmoid(0, EARLY)
         for h in range(1, H):
             sigmoid(h)
         quantize_s(1)
-        finish(1, 0)
-        quantize_q(1, 0)
-        quantize_q(1, 1)
-        products(1)
-        for r in range(1, DEAL):
-            finish(1, r)
-        store(1)
-        invert(2)
-        invert(3)
-        for h in range(2, H):
-            for r in range(DEAL):
-                finish(h, r)
-            store(h)
+        quantize_q(1, 0, HALF)
+        invert(0)
+        invert(1)
+        quantize_q(1, HALF)
+        products(1, range(DEAL // 2))
+        products(1, range(DEAL // 2, DEAL))
+        for h in range(H):
+            for half in range(2):
+                finish(h, 2 * half)
+                if h == 1:
+                    invert(2 + half)
+                finish(h, 2 * half + 1)
+                store(h, half, nc.scalar if h >= 2 and half == 1 else nc.sync)

@@ -127,16 +127,18 @@ def tile_rows_read_relu1_norm_gate_kernel(tc, q, qa, S, og, out):
             cols = slice(half * HALF, (half + 1) * HALF)
             queue.dma_start(out=dealt(out, h)[:, cols], in_=result[h][:, cols])
 
+        nc.sync.dma_start(out=weight[:ROWS, :], in_=qa_rows)
+        nc.scalar.dma_start(out=weight[ROWS:, :], in_=qa_rows)
         nc.scalar.dma_start(out=og_raw[0][:, :EARLY], in_=dealt(og, 0)[:, :EARLY])
         load_q(0, slice(0, 2))
-        for c in range(2):
-            nc.sync.dma_start(out=weight[c * ROWS : (c + 1) * ROWS, :], in_=qa_rows)
         load_q(0, 2)
         load_q(0, 3, 0, HALF)
         load_q(0, 3, HALF)
         load_s(0)
-        for j in range(PACK):
+        for j in range(PACK - 1):
             load_q(1, j)
+        load_q(1, 3, 0, HALF)
+        load_q(1, 3, HALF)
         load_s(1)
         load_og(0, EARLY)
         for h in range(1, H):
@@ -145,14 +147,14 @@ def tile_rows_read_relu1_norm_gate_kernel(tc, q, qa, S, og, out):
         sigmoid(0, 0, EARLY)
         nc.vector.tensor_scalar(out=floor[:], in0=weight[:], scalar1=SHIFT, scalar2=None, op0=ALU.mult)
         nc.vector.tensor_scalar(out=side[:], in0=weight[:], scalar1=0.0, scalar2=0.5, op0=ALU.is_ge, op1=ALU.subtract)
-        affine_vector(0, 0)
         nc.vector.scalar_tensor_tensor(out=low[:], in0=side[:], scalar=FAR, in1=floor[:], op0=ALU.mult, op1=ALU.min)
         nc.vector.scalar_tensor_tensor(out=high[:], in0=side[:], scalar=FAR, in1=floor[:], op0=ALU.mult, op1=ALU.max)
+        affine_vector(0, 0)
         affine_scalar(0, 1)
+        clamp(0, 0)
         affine_vector(0, 2)
         affine_vector(0, 3, HALF)
         affine_scalar(0, 3, HALF)
-        clamp(0, 0)
         clamp(0, 1)
         clamp(0, 2)
         clamp(0, 3, 0, HALF)
@@ -164,30 +166,34 @@ def tile_rows_read_relu1_norm_gate_kernel(tc, q, qa, S, og, out):
             affine_scalar(1, j)
         affine_scalar(1, 3, HALF)
         quantize_s(0)
+        clamp(1, 0)
         quantize_q(0)
         products(0, range(DEAL))
-        clamp(1, 0)
         clamp(1, 1)
         affine_vector(1, 3, HALF)
         clamp(1, 2)
-        clamp(1, 3)
+        clamp(1, 3, 0, HALF)
+        clamp(1, 3, HALF)
         pack_s(1)
-        pack_q(1, DEAL - 1)
+        pack_q(1, DEAL - 1, 0, P // 4)
+        pack_q(1, DEAL - 1, P // 4)
         pack_q_scalar(1, DEAL - 1)
         sigmoid(0, EARLY)
-        for h in range(1, H):
+        for h in range(1, H - 1):
             sigmoid(h)
+        sigmoid(H - 1, 0, HALF)
+        sigmoid(H - 1, HALF)
         quantize_s(1)
-        quantize_q(1, 0, HALF)
         invert(0)
         invert(1)
+        quantize_q(1, 0, HALF)
         quantize_q(1, HALF)
         products(1, range(DEAL // 2))
         products(1, range(DEAL // 2, DEAL))
         for h in range(H):
             for half in range(2):
                 finish(h, 2 * half)
-                if h == 1:
-                    invert(2 + half)
                 finish(h, 2 * half + 1)
+                if half == 0 and h in (1, 2):
+                    invert(h + 1)
                 store(h, half, nc.scalar if h >= 2 and half == 1 else nc.sync)

from contextlib import ExitStack

import concourse.mybir as mybir

H, D, N, E = 4, 256, 512, 128
FLOPS = 2 * H * D * N * E

F32 = mybir.dt.float32
BF16 = mybir.dt.bfloat16
U32 = mybir.dt.uint32
U8 = mybir.dt.uint8
FP8X4 = mybir.dt.float8_e4m3fn_x4
ALU = mybir.AluOpType
ACT = mybir.ActivationFunctionType

P = 128
PACK = 4
ROWS = D // PACK
DEAL = N // P
HALF = N // 2
EARLY = 8
SHIFT = 0.125
FAR = 2.0 ** 127


def tile_rows_read_relu1_norm_gate_kernel(tc, q, qa, S, og, out):
    nc = tc.nc
    q_rows = q.rearrange("h d n -> (h d) n")
    s_rows = S.rearrange("h d e -> (h d) e")
    qa_rows = qa.rearrange("(p j) o -> p (j o)", j=PACK)

    with ExitStack() as ctx:
        sb = ctx.enter_context(tc.tile_pool(name="sb", bufs=1))
        ps = ctx.enter_context(tc.psum_pool(name="ps", bufs=1))
        ctx.enter_context(tc.manual_schedule())

        weight = sb.tile([P, PACK], F32, name="weight")
        floor = sb.tile([P, PACK], F32, name="floor")
        side = sb.tile([P, PACK], F32, name="side")
        low = sb.tile([P, PACK], F32, name="low")
        high = sb.tile([P, PACK], F32, name="high")
        q_raw = [sb.tile([P, PACK, N], F32, name=f"q_raw{g}") for g in range(2)]
        s_raw = [sb.tile([P, PACK, E], F32, name=f"s_raw{g}") for g in range(2)]
        og_raw = [sb.tile([P, N], F32, name=f"og_raw{h}") for h in range(H)]
        gate = [sb.tile([P, N], F32, name=f"gate{h}") for h in range(H)]
        mapped = [sb.tile([P, PACK, N], BF16, name=f"mapped{g}", align_bytes=64) for g in range(2)]
        q_packed = [sb.tile([P, DEAL * P * PACK], BF16, name=f"q_packed{g}", align_bytes=64) for g in range(2)]
        s_packed = [sb.tile([P, E * PACK], BF16, name=f"s_packed{g}", align_bytes=64) for g in range(2)]
        q_codes = [sb.tile([P, N], U32, name=f"q_codes{g}", align_bytes=64) for g in range(2)]
        q_scales = [sb.tile([P, N], U8, name=f"q_scales{g}", align_bytes=64) for g in range(2)]
        s_codes = [sb.tile([P, E], U32, name=f"s_codes{g}", align_bytes=64) for g in range(2)]
        s_scales = [sb.tile([P, E], U8, name=f"s_scales{g}", align_bytes=64) for g in range(2)]
        inverse = [sb.tile([P, DEAL], F32, name=f"inverse{h}") for h in range(H)]
        result = [sb.tile([P, N], F32, name=f"result{h}") for h in range(H)]
        sums = [ps.tile([P, DEAL, E], F32, name=f"sums{h}") for h in range(H)]

        def dealt(x, h):
            return x[h].rearrange("(s r) e -> s (r e)", r=DEAL)

        def load_q(g, places, first=0, last=N):
            src = q_rows[2 * D * g : 2 * D * (g + 1), :].rearrange("(p j) n -> p j n", j=PACK)
            nc.sync.dma_start(out=q_raw[g][:, places, first:last], in_=src[:, places, first:last])

        def load_s(g):
            src = s_rows[2 * D * g : 2 * D * (g + 1), :].rearrange("(p j) e -> p j e", j=PACK)
            nc.sync.dma_start(out=s_raw[g][:], in_=src)

        def load_og(h, first=0):
            nc.sync.dma_start(out=og_raw[h][:, first:], in_=dealt(og, h)[:, first:])

        def sigmoid(h, first=0, last=N):
            nc.scalar.activation(out=gate[h][:, first:last], in_=og_raw[h][:, first:last], func=ACT.Sigmoid)

        def affine_scalar(g, j, first=0):
            nc.scalar.activation(out=mapped[g][:, j, first:], in_=q_raw[g][:, j, first:], func=ACT.Identity,
                                 scale=weight[:, j : j + 1], bias=floor[:, j : j + 1])

        def affine_vector(g, j, last=N):
            nc.vector.tensor_scalar(out=mapped[g][:, j, :last], in0=q_raw[g][:, j, :last], scalar1=SHIFT,
                                    scalar2=weight[:, j : j + 1], op0=ALU.add, op1=ALU.mult)

        def clamp(g, j, first=0, last=N):
            nc.vector.tensor_scalar(out=mapped[g][:, j, first:last], in0=mapped[g][:, j, first:last], scalar1=low[:, j : j + 1],
                                    scalar2=high[:, j : j + 1], op0=ALU.max, op1=ALU.min)

        def pack_q(g, tiles=DEAL, first=0, last=P // 2):
            nc.vector.tensor_copy(
                out=q_packed[g][:].rearrange("p (r a b j) -> p a j b r", r=DEAL, b=2, j=PACK)[:, first:last, :, :, :tiles],
                in_=mapped[g][:].rearrange("p j (a b r) -> p a j b r", b=2, r=DEAL)[:, first:last, :, :, :tiles])

        def pack_q_scalar(g, r):
            nc.scalar.copy(
                out=q_packed[g][:].rearrange("p (r a b j) -> p r a j b", r=DEAL, b=2, j=PACK)[:, r, :, :, :],
                in_=mapped[g][:].rearrange("p j (a b r) -> p r a j b", b=2, r=DEAL)[:, r, :, :, :])

        def pack_s(g):
            nc.scalar.copy(
                out=s_packed[g][:].rearrange("p (c i j) -> p c j i", i=4, j=PACK),
                in_=s_raw[g][:].rearrange("p j (c i) -> p c j i", i=4))

        def quantize_q(g, first=0, last=N):
            nc.vector.quantize_mx(out=q_codes[g][:, first:last].bitcast(FP8X4), scales=q_scales[g][:, first:last],
                                  in_=q_packed[g][:, first * PACK : last * PACK])

        def quantize_s(g):
            nc.vector.quantize_mx(out=s_codes[g][:].bitcast(FP8X4), scales=s_scales[g][:], in_=s_packed[g][:])

        def products(g, tiles):
            for c in range(2):
                for r in tiles:
                    cols = slice(r * P, (r + 1) * P)
                    rows = slice(c * ROWS, (c + 1) * ROWS)
                    nc.tensor.matmul_mx(out=sums[2 * g + c][:, r, :],
                                        lhsT=q_codes[g][rows, cols].bitcast(FP8X4), lhsT_scale=q_scales[g][rows, cols],
                                        rhs=s_codes[g][rows, :].bitcast(FP8X4), rhs_scale=s_scales[g][rows, :],
                                        start=True, stop=True)

        def invert(h):
            nc.vector.reciprocal(out=inverse[h][:], in_=sums[h][:, :, E - 1])

        def finish(h, r):
            cols = slice(r * E, (r + 1) * E)
            nc.vector.scalar_tensor_tensor(out=result[h][:, cols], in0=sums[h][:, r, :], scalar=inverse[h][:, r : r + 1],
                                           in1=gate[h][:, cols], op0=ALU.mult, op1=ALU.mult)

        def store(h, half, queue):
            cols = slice(half * HALF, (half + 1) * HALF)
            queue.dma_start(out=dealt(out, h)[:, cols], in_=result[h][:, cols])

        nc.sync.dma_start(out=weight[:ROWS, :], in_=qa_rows)
        nc.scalar.dma_start(out=weight[ROWS:, :], in_=qa_rows)
        nc.scalar.dma_start(out=og_raw[0][:, :EARLY], in_=dealt(og, 0)[:, :EARLY])
        load_q(0, slice(0, 2))
        load_q(0, 2)
        load_q(0, 3, 0, HALF)
        load_q(0, 3, HALF)
        load_s(0)
        for j in range(PACK - 1):
            load_q(1, j)
        load_q(1, 3, 0, HALF)
        load_q(1, 3, HALF)
        load_s(1)
        load_og(0, EARLY)
        for h in range(1, H):
            load_og(h)

        sigmoid(0, 0, EARLY)
        nc.vector.tensor_scalar(out=floor[:], in0=weight[:], scalar1=SHIFT, scalar2=None, op0=ALU.mult)
        nc.vector.tensor_scalar(out=side[:], in0=weight[:], scalar1=0.0, scalar2=0.5, op0=ALU.is_ge, op1=ALU.subtract)
        nc.vector.scalar_tensor_tensor(out=low[:], in0=side[:], scalar=FAR, in1=floor[:], op0=ALU.mult, op1=ALU.min)
        nc.vector.scalar_tensor_tensor(out=high[:], in0=side[:], scalar=FAR, in1=floor[:], op0=ALU.mult, op1=ALU.max)
        affine_vector(0, 0)
        affine_scalar(0, 1)
        clamp(0, 0)
        affine_vector(0, 2)
        affine_vector(0, 3, HALF)
        affine_scalar(0, 3, HALF)
        clamp(0, 1)
        clamp(0, 2)
        clamp(0, 3, 0, HALF)
        clamp(0, 3, HALF)
        pack_q(0, DEAL, 0, P // 4)
        pack_q(0, DEAL, P // 4)
        pack_s(0)
        for j in range(PACK - 1):
            affine_scalar(1, j)
        affine_scalar(1, 3, HALF)
        quantize_s(0)
        clamp(1, 0)
        quantize_q(0)
        products(0, range(DEAL))
        clamp(1, 1)
        affine_vector(1, 3, HALF)
        clamp(1, 2)
        clamp(1, 3, 0, HALF)
        clamp(1, 3, HALF)
        pack_s(1)
        pack_q(1, DEAL - 1, 0, P // 4)
        pack_q(1, DEAL - 1, P // 4)
        pack_q_scalar(1, DEAL - 1)
        sigmoid(0, EARLY)
        for h in range(1, H - 1):
            sigmoid(h)
        sigmoid(H - 1, 0, HALF)
        sigmoid(H - 1, HALF)
        quantize_s(1)
        invert(0)
        invert(1)
        quantize_q(1, 0, HALF)
        quantize_q(1, HALF)
        products(1, range(DEAL // 2))
        products(1, range(DEAL // 2, DEAL))
        for h in range(H):
            for half in range(2):
                finish(h, 2 * half)
                finish(h, 2 * half + 1)
                if half == 0 and h in (1, 2):
                    invert(h + 1)
                store(h, half, nc.scalar if h >= 2 and half == 1 else nc.sync)
